import numpy as np
import ml_dtypes


def mxq(x, axis, fmt="e4m3"):
    dtype, down = {"e4m3": (ml_dtypes.float8_e4m3fn, 7), "e5m2": (ml_dtypes.float8_e5m2, 14)}[fmt]
    v = np.moveaxis(np.asarray(x, np.float32).astype(ml_dtypes.bfloat16).astype(np.float64), axis, -1)
    blocks = v.reshape(v.shape[:-1] + (-1, 32))
    amax = np.abs(blocks).max(-1, keepdims=True)
    byte = np.maximum(np.where(amax > 0, np.frexp(amax)[1] - 1 + 127, 0) - down, 1)
    scale = np.exp2(byte - 127.0)
    codes = (blocks / scale).astype(np.float32).astype(dtype).astype(np.float64)
    return np.moveaxis((codes * scale).reshape(v.shape), -1, axis)


WIDE = False


def mx_kscale(k):
    if not WIDE:
        return np.ones(k)
    levels = np.array([10, -10, 5, -5, 0])
    if k % 512:
        return np.exp2(np.random.permutation(np.resize(levels, k // 32))).repeat(32)
    a = np.empty((k // 512, 16))
    for p in range(k // 512):
        a[p, :8] = np.random.permutation(np.resize(levels, 8))
        for g in range(8):
            far = levels[np.abs(levels - a[p, g]) >= 10]
            a[p, g + 8] = far[np.random.randint(len(far))]
    return np.exp2(a.ravel()).repeat(32)


def f64(x):
    return np.asarray(x).astype(np.float64)


def striped(idx):
    return np.tile(idx.reshape(-1, 16).T, (8, 1)).astype(np.uint16)


def unstriped(offs):
    return offs[:16].T.reshape(-1).astype(np.int64)


def striped8(idx):
    return np.concatenate([x.reshape(-1, 16).T for x in idx]).astype(np.uint16)


def runs(offs, k):
    lists = np.stack([offs[16 * r : 16 * r + 16].T.reshape(-1) for r in range(8)]).astype(np.int64)
    return lists[np.arange(k) % 512 // 64]


def pack_weight(w):
    k, n = w.shape
    w = f64(np.asarray(w, np.float32).astype(ml_dtypes.bfloat16)).reshape(k // 32, 32, n)
    amax = np.abs(w).max(1)
    byte = np.clip(np.where(amax > 0, np.frexp(amax)[1] - 1 + 127 - 7, 1), 1, 254)
    scaled = (w * np.exp2(127.0 - byte)[:, None, :]).reshape(k, n).astype(np.float32)
    words = np.ascontiguousarray(scaled.reshape(k // 512, 128, 4, n).transpose(0, 1, 3, 2)).astype(ml_dtypes.float8_e4m3fn).view(np.uint8)
    return words, np.ascontiguousarray(byte.astype(np.uint8).reshape(k // 512, 16, n))


def unpack_weight(words, scales):
    g, p, n, _ = words.shape
    vals = np.ascontiguousarray(words).view(ml_dtypes.float8_e4m3fn).astype(np.float64) * np.repeat(np.exp2(scales.astype(np.float64) - 127.0), 8, axis=1)[..., None]
    return vals.transpose(0, 1, 3, 2).reshape(g * 512, n)


K, T, S, H, G = 512, 1024, 512, 512, 2048


def setup_inputs():
    n = np.random.standard_normal
    s = mx_kscale(K)[:, None]
    packed_xT = pack_weight(n((K, T)) * s)
    packed_dT = pack_weight(n((K, G)) / s)
    return {
        "x_words": packed_xT[0],
        "x_scales": packed_xT[1],
        "w1": (n((K, H)) / np.sqrt(K) / s).astype(np.float32),
        "w2": (n((K, H)) / np.sqrt(K) / s).astype(np.float32),
        "gs": (np.random.uniform(0.5, 1.5, (K, 1)) * s).astype(np.float32),
        "d_words": packed_dT[0],
        "d_scales": packed_dT[1],
        "offs": striped(np.random.permutation(T)[:S]),
        "two": striped(np.random.permutation(T)[:S]),
        "n1": striped8(np.stack([np.random.permutation(S) for _ in range(8)])),
        "n2": striped8(np.stack([np.random.permutation(S) for _ in range(8)])),
        "n3": striped8(np.stack([np.random.permutation(S) for _ in range(8)])),
        "k1": striped8(np.random.randint(0, G, (8, H))),
        "n4": striped8(np.stack([np.random.permutation(S) for _ in range(8)])),
        "n5": striped8(np.stack([np.random.permutation(S) for _ in range(8)])),
    }


def reference(x_words, x_scales, w1, w2, gs, d_words, d_scales, offs, two, n1, n2, n3, k1, n4, n5):
    d_k1 = unpack_weight(d_words, d_scales)[np.arange(K)[:, None], runs(k1, K)]
    xq = unpack_weight(x_words, x_scales)[:, unstriped(offs)]
    y = mxq(f64(w1), 0, "e4m3").T @ xq
    x_two = unpack_weight(x_words, x_scales)[:, unstriped(two)]
    d = mxq(f64(w2), 0, "e4m3").T @ x_two
    z = f64(gs) * (np.maximum(np.minimum(y - (0.5 * (y[np.arange(H)[:, None], runs(n1, H)])), d[np.arange(H)[:, None], runs(n2, H)]), d[np.arange(H)[:, None], runs(n3, H)]))
    h = 0.0625 * ((d_k1.T @ mxq(z, 0, "e4m3")))
    st = np.maximum(h, h[np.arange(H)[:, None], runs(n4, H)])
    return st[np.arange(H)[:, None], runs(n5, H)] - (0.5 * h)

@@ -1,0 +1,208 @@
+from contextlib import ExitStack
+
+import concourse.mybir as mybir
+
+F32 = mybir.dt.float32
+BF16 = mybir.dt.bfloat16
+I32 = mybir.dt.int32
+U32 = mybir.dt.uint32
+U16 = mybir.dt.uint16
+U8 = mybir.dt.uint8
+FP8X4 = mybir.dt.float8_e4m3fn_x4
+ALU = mybir.AluOpType
+COPY = mybir.ActivationFunctionType.Copy
+
+P = 128
+PACK = 4
+K, T, S, H, G = 512, 1024, 512, 512, 2048
+HALF = S // 2
+FLOPS = 3 * 2 * K * H * S
+
+
+def tile_picked_twqclampbhopb_none_p_kernel(tc, x_words, x_scales, w1, w2, gs, d_words, d_scales, offs, two, n1, n2, n3, k1, n4, n5, out):
+    nc = tc.nc
+    with ExitStack() as ctx:
+        keep = ctx.enter_context(tc.tile_pool(name="keep", bufs=1))
+        psum = ctx.enter_context(tc.psum_pool(name="psum", bufs=1))
+
+        def sb(name, shape, dtype):
+            return keep.tile(shape, dtype, name=name, align_bytes=64)
+
+        def load_list(name, src):
+            lst = keep.tile([P, S // 16], U16, name=name)
+            nc.sync.dma_start(lst[:], src)
+            return lst
+
+        def load_weight_half(name, w, half):
+            raw = sb(name, [P, PACK, H // 2], F32)
+            cols = slice(half * (H // 2), (half + 1) * (H // 2))
+            nc.sync.dma_start(raw[:], w.rearrange("(p j) c -> p j c", j=PACK)[:, :, cols])
+            return raw
+
+        xs_tab = sb("xs_tab", [P, T], U8)
+        ds_tab = sb("ds_tab", [P, G], U8)
+        dq_scales = sb("dq_scales", [P, H], U8)
+        nc.vector.memset(xs_tab[:].bitcast(I32), 0)
+        nc.gpsimd.memset(ds_tab[:].bitcast(I32), 0)
+        nc.gpsimd.memset(dq_scales[:].bitcast(I32), 0)
+
+        offs_l = load_list("offs_l", offs)
+        for q in range(4):
+            nc.sync.dma_start(xs_tab[32 * q : 32 * q + 4, :].bitcast(I32), x_scales[0, 4 * q : 4 * q + 4, :].bitcast(I32))
+        two_l = load_list("two_l", two)
+        xw_tab = sb("xw_tab", [P, T], I32)
+        nc.sync.dma_start(xw_tab[:], x_words[0].rearrange("p n r -> p (n r)").bitcast(I32))
+        w1_raw = [load_weight_half("w1_raw%d" % h, w1, h) for h in range(2)]
+        k1_l = load_list("k1_l", k1)
+        nc.sync.dma_start(ds_tab[0:P:8, :].bitcast(I32), d_scales[0].bitcast(I32))
+        n1_l = load_list("n1_l", n1)
+        w2_raw = [load_weight_half("w2_raw%d" % h, w2, h) for h in range(2)]
+        dw_tab = sb("dw_tab", [P, G], I32)
+        nc.sync.dma_start(dw_tab[:], d_words[0].rearrange("p n r -> p (n r)").bitcast(I32))
+        n2_l = load_list("n2_l", n2)
+        n3_l = load_list("n3_l", n3)
+        gs_sb = sb("gs_sb", [P, PACK], F32)
+        nc.sync.dma_start(gs_sb[:], gs.rearrange("(p t) o -> p (t o)", t=PACK))
+        n4_l = load_list("n4_l", n4)
+        n5_l = load_list("n5_l", n5)
+
+        def gather_bytes(name, table, lst):
+            got = sb(name, [P, S], U8)
+            nc.vector.tensor_copy(got[:], table[:].indirect(lst[:]))
+            return got
+
+        def gather_words(name, table, lst):
+            got = sb(name, [P, S], U32)
+            nc.vector.tensor_copy(got[:], table[:].bitcast(U32).indirect(lst[:]))
+            return got
+
+        xa_scales = gather_bytes("xa_scales", xs_tab, offs_l)
+        xb_scales = gather_bytes("xb_scales", xs_tab, two_l)
+        xa_words = gather_words("xa_words", xw_tab, offs_l)
+        xb_words = gather_words("xb_words", xw_tab, two_l)
+
+        def cast_weight(name, raw):
+            grouped = sb(name, [P, H * PACK], BF16)
+            view = grouped[:].rearrange("p (t m j) -> p m t j", t=PACK, j=PACK)
+            for h in range(2):
+                nc.scalar.activation(view[:, 64 * h : 64 * (h + 1)], raw[h][:].rearrange("p j (m t) -> p m t j", t=PACK), COPY)
+            return grouped
+
+        def quantize(name, grouped, width):
+            codes = sb(name + "_codes", [P, width], U32)
+            scales = sb(name + "_scales", [P, width], U8)
+            nc.vector.quantize_mx(out=codes[:].bitcast(FP8X4), scales=scales[:], in_=grouped[:])
+            return codes, scales
+
+        def product(tag, t, lhs, lhs_scales, rhs, rhs_scales, width):
+            acc = psum.tile([P, S], F32, name=tag, tag=tag)
+            cols = slice(P * t, P * (t + 1))
+            nc.tensor.matmul_mx(out=acc[:, 0:width], lhsT=lhs[:, cols].bitcast(FP8X4), lhsT_scale=lhs_scales[:, cols],
+                                rhs=rhs[:].bitcast(FP8X4), rhs_scale=rhs_scales[:], start=True, stop=True)
+            return acc
+
+        win_a = [sb("win_a%d" % t, [P, 2 * S], F32) for t in range(PACK)]
+        win_b = [sb("win_b%d" % t, [P, 2 * S], F32) for t in range(PACK)]
+
+        w1_grouped = cast_weight("w1_grouped", w1_raw)
+        w1_codes, w1_scales = quantize("w1", w1_grouped, H)
+
+        dg_scales = gather_bytes("dg_scales", ds_tab, k1_l)
+        dd_scales = sb("dd_scales", [P, H], U8)
+        nc.vector.tensor_copy(dd_scales[:].rearrange("p (t a b) -> p a t b", t=PACK, b=4), dg_scales[:].rearrange("p (a b t) -> p a t b", t=PACK, b=4))
+        for r in range(4):
+            nc.sync.dma_start(dq_scales[r:P:32, :].bitcast(I32), dd_scales[8 * r : P : 32, :].bitcast(I32))
+
+        y_acc = [product("bank_a%d" % t, t, w1_codes, w1_scales, xa_words, xa_scales, S) for t in range(PACK)]
+
+        def leave_y(t):
+            nc.scalar.activation(win_b[t][:, S:], y_acc[t][:], COPY)
+            nc.scalar.activation(win_a[t][:, 0:S], y_acc[t][:], COPY, scale=-0.5)
+
+        leave_y(0)
+        w2_grouped = cast_weight("w2_grouped", w2_raw)
+        w2_codes, w2_scales = quantize("w2", w2_grouped, H)
+        d_acc = [product("bank_b%d" % t, t, w2_codes, w2_scales, xb_words, xb_scales, S) for t in range(PACK)]
+
+        u = [sb("u%d" % t, [P, S], F32) for t in range(PACK)]
+        ga = [sb("ga%d" % t, [P, S], F32) for t in range(PACK)]
+        gb = [sb("gb%d" % t, [P, S], F32) for t in range(PACK)]
+        lo = [sb("lo%d" % t, [P, S], F32) for t in range(PACK)]
+        zf = [sb("zf%d" % t, [P, S], F32) for t in range(PACK)]
+        z_grouped = [sb("z_grouped%d" % c, [P, HALF * PACK], BF16) for c in range(2)]
+
+        def step_u(t):
+            nc.vector.tensor_tensor(u[t][:], win_a[t][:].indirect(n1_l[:]), win_b[t][:, S:], ALU.add)
+
+        def step_a(t):
+            nc.vector.tensor_copy(ga[t][:], win_b[t][:].indirect(n2_l[:]))
+
+        def step_min(t):
+            nc.vector.tensor_tensor(lo[t][:], u[t][:], ga[t][:], ALU.min)
+
+        def step_b(t, c0, c1):
+            nc.vector.tensor_copy(gb[t][:, c0:c1], win_b[t][:].indirect(n3_l[:, c0 // 16 : c1 // 16]))
+
+        def step_max(t, c0, c1):
+            nc.vector.tensor_tensor(zf[t][:, c0:c1], lo[t][:, c0:c1], gb[t][:, c0:c1], ALU.max)
+            for c in range(c0 // HALF, c1 // HALF):
+                nc.scalar.activation(z_grouped[c][:].rearrange("p (n t) -> p t n", t=PACK)[:, t, :], zf[t][:, c * HALF : (c + 1) * HALF], COPY, scale=gs_sb[:, t : t + 1])
+
+        step_u(0)
+        leave_y(1)
+        step_u(1)
+        dg_words = gather_words("dg_words", dw_tab, k1_l)
+        dq_words = sb("dq_words", [P, H], U32)
+        nc.vector.tensor_copy(dq_words[:].rearrange("p (t a b) -> p a t b", t=PACK, b=4), dg_words[:].rearrange("p (a b t) -> p a t b", t=PACK, b=4))
+        for t in range(PACK):
+            nc.scalar.activation(win_b[t][:, 0:S], d_acc[t][:], COPY)
+            if t + 2 < PACK:
+                leave_y(t + 2)
+        for t in range(PACK - 1):
+            step_a(t)
+            step_b(t, 0, S)
+            step_min(t)
+            if t + 2 < PACK:
+                step_u(t + 2)
+            else:
+                step_a(t + 1)
+            step_max(t, 0, S)
+        last = PACK - 1
+        step_b(last, 0, HALF)
+        step_min(last)
+        step_b(last, HALF, S)
+        step_max(last, 0, HALF)
+        step_max(last, HALF, S)
+
+        zq = [quantize("z%d" % c, z_grouped[c], HALF) for c in range(2)]
+        h_acc = [[product(("bank_a%d", "bank_b%d")[c] % t, t, dq_words, dq_scales, zq[c][0], zq[c][1], HALF) for t in range(PACK)] for c in range(2)]
+        half_h = [sb("half_h%d" % t, [P, S], F32) for t in range(PACK)]
+        for t in range(PACK):
+            for c in range(2):
+                nc.scalar.activation(win_a[t][:, c * HALF : (c + 1) * HALF], h_acc[c][t][:, 0:HALF], COPY, scale=0.0625)
+        for t in range(PACK):
+            nc.scalar.activation(half_h[t][:], win_a[t][:, 0:S], COPY, scale=0.5)
+
+        gh = [sb("gh%d" % t, [P, S], F32) for t in range(PACK)]
+        res = [sb("res%d" % t, [P, S], F32) for t in range(PACK)]
+        out_rows = out.rearrange("(p t) n -> t p n", t=PACK)
+
+        def step_h(t):
+            nc.vector.tensor_copy(gh[t][:], win_a[t][:].indirect(n4_l[:]))
+
+        def step_st(t):
+            nc.vector.tensor_tensor(win_b[t][:, 0:S], win_a[t][:, 0:S], gh[t][:], ALU.max)
+
+        def step_out(t, c0, c1):
+            nc.vector.tensor_tensor(res[t][:, c0:c1], win_b[t][:].indirect(n5_l[:, c0 // 16 : c1 // 16]), half_h[t][:, c0:c1], ALU.subtract)
+            nc.sync.dma_start(out_rows[t][:, c0:c1], res[t][:, c0:c1])
+
+        step_h(0)
+        for t in range(PACK):
+            if t + 1 < PACK:
+                step_h(t + 1)
+            step_st(t)
+            if t >= 1:
+                step_out(t - 1, 0, S)
+        step_out(last, 0, HALF)
+        step_out(last, HALF, S)

@@ -1,6 +1,7 @@
 from contextlib import ExitStack
 
 import concourse.mybir as mybir
+from concourse.masks import make_identity
 
 F32 = mybir.dt.float32
 BF16 = mybir.dt.bfloat16
@@ -11,6 +12,7 @@ U8 = mybir.dt.uint8
 FP8X4 = mybir.dt.float8_e4m3fn_x4
 ALU = mybir.AluOpType
 COPY = mybir.ActivationFunctionType.Copy
+RELU = mybir.ActivationFunctionType.Relu
 
 P = 128
 PACK = 4
@@ -25,8 +27,8 @@ def tile_picked_twqclampbhopb_none_p_kernel(tc, x_words, x_scales, w1, w2, gs, d
         keep = ctx.enter_context(tc.tile_pool(name="keep", bufs=1))
         psum = ctx.enter_context(tc.psum_pool(name="psum", bufs=1))
 
-        def sb(name, shape, dtype):
-            return keep.tile(shape, dtype, name=name, align_bytes=64)
+        def sb(name, shape, dtype, tag=None):
+            return keep.tile(shape, dtype, name=name, tag=tag or name, align_bytes=64)
 
         def load_list(name, src):
             lst = keep.tile([P, S // 16], U16, name=name)
@@ -42,9 +44,12 @@ def tile_picked_twqclampbhopb_none_p_kernel(tc, x_words, x_scales, w1, w2, gs, d
         xs_tab = sb("xs_tab", [P, T], U8)
         ds_tab = sb("ds_tab", [P, G], U8)
         dq_scales = sb("dq_scales", [P, H], U8)
-        nc.vector.memset(xs_tab[:].bitcast(I32), 0)
+        nc.gpsimd.memset(xs_tab[:].bitcast(I32), 0)
         nc.gpsimd.memset(ds_tab[:].bitcast(I32), 0)
         nc.gpsimd.memset(dq_scales[:].bitcast(I32), 0)
+
+        ident = sb("ident", [P, P], F32)
+        make_identity(nc, ident[:])
 
         offs_l = load_list("offs_l", offs)
         for q in range(4):
@@ -53,16 +58,16 @@ def tile_picked_twqclampbhopb_none_p_kernel(tc, x_words, x_scales, w1, w2, gs, d
         xw_tab = sb("xw_tab", [P, T], I32)
         nc.sync.dma_start(xw_tab[:], x_words[0].rearrange("p n r -> p (n r)").bitcast(I32))
         w1_raw = [load_weight_half("w1_raw%d" % h, w1, h) for h in range(2)]
-        k1_l = load_list("k1_l", k1)
-        nc.sync.dma_start(ds_tab[0:P:8, :].bitcast(I32), d_scales[0].bitcast(I32))
         n1_l = load_list("n1_l", n1)
         w2_raw = [load_weight_half("w2_raw%d" % h, w2, h) for h in range(2)]
-        dw_tab = sb("dw_tab", [P, G], I32)
-        nc.sync.dma_start(dw_tab[:], d_words[0].rearrange("p n r -> p (n r)").bitcast(I32))
+        k1_l = load_list("k1_l", k1)
+        nc.sync.dma_start(ds_tab[0:P:8, :].bitcast(I32), d_scales[0].bitcast(I32))
         n2_l = load_list("n2_l", n2)
         n3_l = load_list("n3_l", n3)
         gs_sb = sb("gs_sb", [P, PACK], F32)
         nc.sync.dma_start(gs_sb[:], gs.rearrange("(p t) o -> p (t o)", t=PACK))
+        dw_tab = sb("dw_tab", [P, G], I32)
+        nc.sync.dma_start(dw_tab[:], d_words[0].rearrange("p n r -> p (n r)").bitcast(I32))
         n4_l = load_list("n4_l", n4)
         n5_l = load_list("n5_l", n5)
 
@@ -71,21 +76,21 @@ def tile_picked_twqclampbhopb_none_p_kernel(tc, x_words, x_scales, w1, w2, gs, d
             nc.vector.tensor_copy(got[:], table[:].indirect(lst[:]))
             return got
 
-        def gather_words(name, table, lst):
-            got = sb(name, [P, S], U32)
-            nc.vector.tensor_copy(got[:], table[:].bitcast(U32).indirect(lst[:]))
+        def gather_words(name, table, entries, count, tag=None):
+            got = sb(name, [P, count], U32, tag)
+            nc.vector.tensor_copy(got[:], table[:].bitcast(U32).indirect(entries))
             return got
 
         xa_scales = gather_bytes("xa_scales", xs_tab, offs_l)
         xb_scales = gather_bytes("xb_scales", xs_tab, two_l)
-        xa_words = gather_words("xa_words", xw_tab, offs_l)
-        xb_words = gather_words("xb_words", xw_tab, two_l)
+        xa_words = gather_words("xa_words", xw_tab, offs_l[:], S)
+        xb_words = gather_words("xb_words", xw_tab, two_l[:], S)
 
         def cast_weight(name, raw):
             grouped = sb(name, [P, H * PACK], BF16)
             view = grouped[:].rearrange("p (t m j) -> p m t j", t=PACK, j=PACK)
             for h in range(2):
-                nc.scalar.activation(view[:, 64 * h : 64 * (h + 1)], raw[h][:].rearrange("p j (m t) -> p m t j", t=PACK), COPY)
+                nc.scalar.activation(view[:, 64 * h : 64 * (h + 1)], raw[h].rearrange("p j (m t) -> p m t j", t=PACK), COPY)
             return grouped
 
         def quantize(name, grouped, width):
@@ -98,13 +103,13 @@ def tile_picked_twqclampbhopb_none_p_kernel(tc, x_words, x_scales, w1, w2, gs, d
             acc = psum.tile([P, S], F32, name=tag, tag=tag)
             cols = slice(P * t, P * (t + 1))
             nc.tensor.matmul_mx(out=acc[:, 0:width], lhsT=lhs[:, cols].bitcast(FP8X4), lhsT_scale=lhs_scales[:, cols],
-                                rhs=rhs[:].bitcast(FP8X4), rhs_scale=rhs_scales[:], start=True, stop=True)
+                                rhs=rhs.bitcast(FP8X4), rhs_scale=rhs_scales, start=True, stop=True)
             return acc
 
         win_a = [sb("win_a%d" % t, [P, 2 * S], F32) for t in range(PACK)]
         win_b = [sb("win_b%d" % t, [P, 2 * S], F32) for t in range(PACK)]
 
-        w1_grouped = cast_weight("w1_grouped", w1_raw)
+        w1_grouped = cast_weight("w1_grouped", [r[:] for r in w1_raw])
         w1_codes, w1_scales = quantize("w1", w1_grouped, H)
 
         dg_scales = gather_bytes("dg_scales", ds_tab, k1_l)
@@ -113,96 +118,144 @@ def tile_picked_twqclampbhopb_none_p_kernel(tc, x_words, x_scales, w1, w2, gs, d
         for r in range(4):
             nc.sync.dma_start(dq_scales[r:P:32, :].bitcast(I32), dd_scales[8 * r : P : 32, :].bitcast(I32))
 
-        y_acc = [product("bank_a%d" % t, t, w1_codes, w1_scales, xa_words, xa_scales, S) for t in range(PACK)]
+        y_acc = [product("bank_a%d" % t, t, w1_codes, w1_scales, xa_words[:], xa_scales[:], S) for t in range(PACK)]
 
         def leave_y(t):
             nc.scalar.activation(win_b[t][:, S:], y_acc[t][:], COPY)
             nc.scalar.activation(win_a[t][:, 0:S], y_acc[t][:], COPY, scale=-0.5)
 
-        leave_y(0)
-        w2_grouped = cast_weight("w2_grouped", w2_raw)
+        w2_grouped = cast_weight("w2_grouped", [r[:] for r in w2_raw])
         w2_codes, w2_scales = quantize("w2", w2_grouped, H)
-        d_acc = [product("bank_b%d" % t, t, w2_codes, w2_scales, xb_words, xb_scales, S) for t in range(PACK)]
+        d_acc = [product("bank_b%d" % t, t, w2_codes, w2_scales, xb_words[:], xb_scales[:], S) for t in range(PACK)]
 
-        u = [sb("u%d" % t, [P, S], F32) for t in range(PACK)]
-        ga = [sb("ga%d" % t, [P, S], F32) for t in range(PACK)]
-        gb = [sb("gb%d" % t, [P, S], F32) for t in range(PACK)]
+        u, ga = {}, {}
         lo = [sb("lo%d" % t, [P, S], F32) for t in range(PACK)]
-        zf = [sb("zf%d" % t, [P, S], F32) for t in range(PACK)]
         z_grouped = [sb("z_grouped%d" % c, [P, HALF * PACK], BF16) for c in range(2)]
 
+        def turn(tag, terms):
+            acc = psum.tile([P, S], F32, name="turned", tag=tag)
+            for c in range(S // P):
+                cols = slice(P * c, P * (c + 1))
+                for i, term in enumerate(terms):
+                    nc.tensor.matmul(acc[:, cols], lhsT=term[:, cols], rhs=ident[:], is_transpose=True, start=i == 0, stop=i == len(terms) - 1)
+            return acc
+
         def step_u(t):
+            u[t] = sb("u%d" % t, [P, S], F32, None)
             nc.vector.tensor_tensor(u[t][:], win_a[t][:].indirect(n1_l[:]), win_b[t][:, S:], ALU.add)
 
         def step_a(t):
+            ga[t] = sb("ga%d" % t, [P, S], F32)
             nc.vector.tensor_copy(ga[t][:], win_b[t][:].indirect(n2_l[:]))
 
-        def step_min(t):
-            nc.vector.tensor_tensor(lo[t][:], u[t][:], ga[t][:], ALU.min)
+        def step_min(t, c0, c1):
+            nc.vector.tensor_tensor(lo[t][:, c0:c1], u[t][:, c0:c1], ga[t][:, c0:c1], ALU.min)
 
-        def step_b(t, c0, c1):
-            nc.vector.tensor_copy(gb[t][:, c0:c1], win_b[t][:].indirect(n3_l[:, c0 // 16 : c1 // 16]))
-
-        def step_max(t, c0, c1):
-            nc.vector.tensor_tensor(zf[t][:, c0:c1], lo[t][:, c0:c1], gb[t][:, c0:c1], ALU.max)
+        def leave_z(t, values, c0, c1):
             for c in range(c0 // HALF, c1 // HALF):
-                nc.scalar.activation(z_grouped[c][:].rearrange("p (n t) -> p t n", t=PACK)[:, t, :], zf[t][:, c * HALF : (c + 1) * HALF], COPY, scale=gs_sb[:, t : t + 1])
+                nc.scalar.activation(z_grouped[c][:].rearrange("p (n t) -> p t n", t=PACK)[:, t, :], values[:, c * HALF : (c + 1) * HALF], COPY, scale=gs_sb[:, t : t + 1])
 
-        step_u(0)
-        leave_y(1)
-        step_u(1)
-        dg_words = gather_words("dg_words", dw_tab, k1_l)
-        dq_words = sb("dq_words", [P, H], U32)
-        nc.vector.tensor_copy(dq_words[:].rearrange("p (t a b) -> p a t b", t=PACK, b=4), dg_words[:].rearrange("p (a b t) -> p a t b", t=PACK, b=4))
-        for t in range(PACK):
-            nc.scalar.activation(win_b[t][:, 0:S], d_acc[t][:], COPY)
-            if t + 2 < PACK:
-                leave_y(t + 2)
-        for t in range(PACK - 1):
-            step_a(t)
-            step_b(t, 0, S)
-            step_min(t)
-            if t + 2 < PACK:
-                step_u(t + 2)
-            else:
-                step_a(t + 1)
-            step_max(t, 0, S)
+        def step_b(t, c0, c1, tag):
+            got = sb("gb%d_%d" % (t, c0), [P, c1 - c0], F32, tag)
+            nc.vector.tensor_copy(got[:], win_b[t][:].indirect(n3_l[:, c0 // 16 : c1 // 16]))
+            return got
+
+        def step_max(t, c0, c1, floor, zf):
+            nc.vector.tensor_tensor(zf[:, c0:c1], lo[t][:, c0:c1], floor[:], ALU.max)
+            leave_z(t, zf, c0, c1)
+
+        dg_lo = gather_words("dg_lo", dw_tab, k1_l[:, 0:16], HALF)
         last = PACK - 1
-        step_b(last, 0, HALF)
-        step_min(last)
-        step_b(last, HALF, S)
-        step_max(last, 0, HALF)
-        step_max(last, HALF, S)
+        for t in range(PACK):
+            leave_y(t)
+            nc.scalar.activation(win_b[t][:, 0:S], d_acc[t][:], COPY)
+        zf = [sb("zf%d" % t, [P, S], F32) for t in range(PACK)]
+        step_u(0)
+        for t in range(last):
+            step_a(t)
+            floor = step_b(t, 0, S, None)
+            step_min(t, 0, S)
+            step_u(t + 1)
+            step_max(t, 0, S, floor, zf[t])
+        step_a(last)
+        floor_a = step_b(last, 0, HALF, None)
+        step_min(last, 0, HALF)
+        step_min(last, HALF, S)
+        step_max(last, 0, HALF, floor_a, zf[last])
+        floor_b = step_b(last, HALF, S, "ga3")
+        dq_words = sb("dq_words", [P, H], U32, "gb3_0")
+        dealt = dq_words[:].rearrange("p (t a b) -> p a t b", t=PACK, b=4)
+        nc.vector.tensor_copy(dealt[:, 0:16], dg_lo[:].rearrange("p (a b t) -> p a t b", t=PACK, b=4))
+        step_max(last, HALF, S, floor_b, zf[last])
 
-        zq = [quantize("z%d" % c, z_grouped[c], HALF) for c in range(2)]
-        h_acc = [[product(("bank_a%d", "bank_b%d")[c] % t, t, dq_words, dq_scales, zq[c][0], zq[c][1], HALF) for t in range(PACK)] for c in range(2)]
+        dg_hi = gather_words("dg_hi", dw_tab, k1_l[:, 16:32], HALF, "win_b3")
+        z_codes = sb("z_codes", [P, S], U32)
+        z_scales = sb("z_scales", [P, S], U8)
+
+        def quantize_z(c):
+            cols = slice(c * HALF, (c + 1) * HALF)
+            nc.vector.quantize_mx(out=z_codes[:, cols].bitcast(FP8X4), scales=z_scales[:, cols], in_=z_grouped[c][:])
+
+        quantize_z(0)
+        picked = dg_hi[:].rearrange("p (a b t) -> p a t b", t=PACK, b=4)
+        nc.vector.tensor_copy(dealt[:, 16:32, 0:1, :], picked[:, :, 0:1, :])
+        quantize_z(1)
+        nc.vector.tensor_copy(dealt[:, 16:32, 1:PACK, :], picked[:, :, 1:PACK, :])
+        h_first = [product(("bank_a0", "bank_b0")[c], 0, dq_words, dq_scales, z_codes[:, c * HALF : (c + 1) * HALF], z_scales[:, c * HALF : (c + 1) * HALF], HALF) for c in range(2)]
+        h_acc = {t: product("bank_a%d" % t, t, dq_words, dq_scales, z_codes[:], z_scales[:], S) for t in range(1, PACK)}
+        win_h = [sb("win_h%d" % t, [P, 2 * S], F32) for t in range(PACK)]
+        win_st = [sb("win_st%d" % t, [P, 2 * S], F32, "win_h2" if t == 0 else None) for t in range(PACK)]
         half_h = [sb("half_h%d" % t, [P, S], F32) for t in range(PACK)]
-        for t in range(PACK):
-            for c in range(2):
-                nc.scalar.activation(win_a[t][:, c * HALF : (c + 1) * HALF], h_acc[c][t][:, 0:HALF], COPY, scale=0.0625)
-        for t in range(PACK):
-            nc.scalar.activation(half_h[t][:], win_a[t][:, 0:S], COPY, scale=0.5)
-
         gh = [sb("gh%d" % t, [P, S], F32) for t in range(PACK)]
         res = [sb("res%d" % t, [P, S], F32) for t in range(PACK)]
         out_rows = out.rearrange("(p t) n -> t p n", t=PACK)
+        direct, turned = (0, 3), (1, 2)
+
+        def leave_h(t):
+            nc.scalar.activation(win_h[t][:, 0:S], h_acc[t][:], COPY, scale=0.0625 if t in direct else 0.03125)
+
+        def halve(t):
+            nc.scalar.activation(half_h[t][:], win_h[t][:, 0:S], COPY, scale=0.5 if t in direct else 1.0)
 
         def step_h(t):
-            nc.vector.tensor_copy(gh[t][:], win_a[t][:].indirect(n4_l[:]))
+            nc.vector.tensor_copy(gh[t][:], win_h[t][:].indirect(n4_l[:]))
+
+        def step_gap(t):
+            nc.vector.tensor_tensor(gh[t][:], win_h[t][:].indirect(n4_l[:]), half_h[t][:], ALU.subtract)
 
         def step_st(t):
-            nc.vector.tensor_tensor(win_b[t][:, 0:S], win_a[t][:, 0:S], gh[t][:], ALU.max)
+            nc.vector.tensor_tensor(win_st[t][:, 0:S], win_h[t][:, 0:S], gh[t][:], ALU.max)
 
         def step_out(t, c0, c1):
-            nc.vector.tensor_tensor(res[t][:, c0:c1], win_b[t][:].indirect(n5_l[:, c0 // 16 : c1 // 16]), half_h[t][:, c0:c1], ALU.subtract)
+            nc.vector.tensor_tensor(res[t][:, c0:c1], win_st[t][:].indirect(n5_l[:, c0 // 16 : c1 // 16]), half_h[t][:, c0:c1], ALU.subtract)
             nc.sync.dma_start(out_rows[t][:, c0:c1], res[t][:, c0:c1])
 
+        for c in range(2):
+            nc.scalar.activation(win_h[0][:, c * HALF : (c + 1) * HALF], h_first[c][:, 0:HALF], COPY, scale=0.0625)
         step_h(0)
-        for t in range(PACK):
-            if t + 1 < PACK:
-                step_h(t + 1)
+        for t in turned:
+            leave_h(t)
+            halve(t)
+            step_gap(t)
+        leave_h(last)
+        step_h(last)
+        rise = {}
+        for t in turned:
+            rise[t] = sb("rise%d" % t, [P, S], F32)
+            nc.scalar.activation(rise[t][:], gh[t][:], RELU)
+        for t in direct:
             step_st(t)
-            if t >= 1:
-                step_out(t - 1, 0, S)
-        step_out(last, 0, HALF)
-        step_out(last, HALF, S)
+        halve(0)
+        summed = {}
+        for t in turned:
+            acc = turn("bank_a%d" % t, [half_h[t], rise[t]])
+            summed[t] = sb("summed%d" % t, [P, S], F32)
+            nc.scalar.activation(summed[t][:], acc[:], COPY, scale=2.0)
+        halve(last)
+        for t in turned:
+            acc = turn("bank_b%d" % t, [summed[t]])
+            nc.scalar.activation(win_st[t][:, 0:S], acc[:], COPY)
+        for t in direct + turned[:-1]:
+            step_out(t, 0, S)
+        step_out(turned[-1], 0, HALF)
+        step_out(turned[-1], HALF, S)

@@ -88,9 +88,9 @@ def tile_picked_twqclampbhopb_none_p_kernel(tc, x_words, x_scales, w1, w2, gs, d
 
         def cast_weight(name, raw):
             grouped = sb(name, [P, H * PACK], BF16)
-            view = grouped[:].rearrange("p (t m j) -> p m t j", t=PACK, j=PACK)
+            view = grouped[:].rearrange("p (t m j) -> p m j t", t=PACK, j=PACK)
             for h in range(2):
-                nc.scalar.activation(view[:, 64 * h : 64 * (h + 1)], raw[h].rearrange("p j (m t) -> p m t j", t=PACK), COPY)
+                nc.scalar.activation(view[:, 64 * h : 64 * (h + 1)], raw[h].rearrange("p j (m t) -> p m j t", t=PACK), COPY)
             return grouped
 
         def quantize(name, grouped, width):
@@ -114,7 +114,7 @@ def tile_picked_twqclampbhopb_none_p_kernel(tc, x_words, x_scales, w1, w2, gs, d
 
         dg_scales = gather_bytes("dg_scales", ds_tab, k1_l)
         dd_scales = sb("dd_scales", [P, H], U8)
-        nc.vector.tensor_copy(dd_scales[:].rearrange("p (t a b) -> p a t b", t=PACK, b=4), dg_scales[:].rearrange("p (a b t) -> p a t b", t=PACK, b=4))
+        nc.vector.tensor_copy(dd_scales[:].rearrange("p (t m) -> p m t", t=PACK), dg_scales[:].rearrange("p (m t) -> p m t", t=PACK))
         for r in range(4):
             nc.sync.dma_start(dq_scales[r:P:32, :].bitcast(I32), dd_scales[8 * r : P : 32, :].bitcast(I32))
 
@@ -184,8 +184,8 @@ def tile_picked_twqclampbhopb_none_p_kernel(tc, x_words, x_scales, w1, w2, gs, d
         step_max(last, 0, HALF, floor_a, zf[last])
         floor_b = step_b(last, HALF, S, "ga3")
         dq_words = sb("dq_words", [P, H], U32, "gb3_0")
-        dealt = dq_words[:].rearrange("p (t a b) -> p a t b", t=PACK, b=4)
-        nc.vector.tensor_copy(dealt[:, 0:16], dg_lo[:].rearrange("p (a b t) -> p a t b", t=PACK, b=4))
+        dealt = dq_words[:].rearrange("p (t m) -> p m t", t=PACK)
+        nc.vector.tensor_copy(dealt[:, 0:64], dg_lo[:].rearrange("p (m t) -> p m t", t=PACK))
         step_max(last, HALF, S, floor_b, zf[last])
 
         dg_hi = gather_words("dg_hi", dw_tab, k1_l[:, 16:32], HALF, "win_b3")
@@ -197,10 +197,10 @@ def tile_picked_twqclampbhopb_none_p_kernel(tc, x_words, x_scales, w1, w2, gs, d
             nc.vector.quantize_mx(out=z_codes[:, cols].bitcast(FP8X4), scales=z_scales[:, cols], in_=z_grouped[c][:])
 
         quantize_z(0)
-        picked = dg_hi[:].rearrange("p (a b t) -> p a t b", t=PACK, b=4)
-        nc.vector.tensor_copy(dealt[:, 16:32, 0:1, :], picked[:, :, 0:1, :])
+        picked = dg_hi[:].rearrange("p (m t) -> p m t", t=PACK)
+        nc.vector.tensor_copy(dealt[:, 64:128, 0:1], picked[:, :, 0:1])
         quantize_z(1)
-        nc.vector.tensor_copy(dealt[:, 16:32, 1:PACK, :], picked[:, :, 1:PACK, :])
+        nc.vector.tensor_copy(dealt[:, 64:128, 1:PACK], picked[:, :, 1:PACK])
         h_first = [product(("bank_a0", "bank_b0")[c], 0, dq_words, dq_scales, z_codes[:, c * HALF : (c + 1) * HALF], z_scales[:, c * HALF : (c + 1) * HALF], HALF) for c in range(2)]
         h_acc = {t: product("bank_a%d" % t, t, dq_words, dq_scales, z_codes[:], z_scales[:], S) for t in range(1, PACK)}
         win_h = [sb("win_h%d" % t, [P, 2 * S], F32) for t in range(PACK)]

from contextlib import ExitStack

import concourse.mybir as mybir
from concourse.masks import make_identity

F32 = mybir.dt.float32
BF16 = mybir.dt.bfloat16
I32 = mybir.dt.int32
U32 = mybir.dt.uint32
U16 = mybir.dt.uint16
U8 = mybir.dt.uint8
FP8X4 = mybir.dt.float8_e4m3fn_x4
ALU = mybir.AluOpType
COPY = mybir.ActivationFunctionType.Copy
RELU = mybir.ActivationFunctionType.Relu

P = 128
PACK = 4
K, T, S, H, G = 512, 1024, 512, 512, 2048
HALF = S // 2
FLOPS = 3 * 2 * K * H * S


def tile_picked_twqclampbhopb_none_p_kernel(tc, x_words, x_scales, w1, w2, gs, d_words, d_scales, offs, two, n1, n2, n3, k1, n4, n5, out):
    nc = tc.nc
    with ExitStack() as ctx:
        keep = ctx.enter_context(tc.tile_pool(name="keep", bufs=1))
        psum = ctx.enter_context(tc.psum_pool(name="psum", bufs=1))

        def sb(name, shape, dtype, tag=None):
            return keep.tile(shape, dtype, name=name, tag=tag or name, align_bytes=64)

        def load_list(name, src):
            lst = keep.tile([P, S // 16], U16, name=name)
            nc.sync.dma_start(lst[:], src)
            return lst

        def load_weight_half(name, w, half):
            raw = sb(name, [P, PACK, H // 2], F32)
            cols = slice(half * (H // 2), (half + 1) * (H // 2))
            nc.sync.dma_start(raw[:], w.rearrange("(p j) c -> p j c", j=PACK)[:, :, cols])
            return raw

        xs_tab = sb("xs_tab", [P, T], U8)
        ds_tab = sb("ds_tab", [P, G], U8)
        dq_scales = sb("dq_scales", [P, H], U8)
        nc.gpsimd.memset(xs_tab[:].bitcast(I32), 0)
        nc.gpsimd.memset(ds_tab[:].bitcast(I32), 0)
        nc.gpsimd.memset(dq_scales[:].bitcast(I32), 0)

        ident = sb("ident", [P, P], F32)
        make_identity(nc, ident[:])

        offs_l = load_list("offs_l", offs)
        for q in range(4):
            nc.sync.dma_start(xs_tab[32 * q : 32 * q + 4, :].bitcast(I32), x_scales[0, 4 * q : 4 * q + 4, :].bitcast(I32))
        two_l = load_list("two_l", two)
        xw_tab = sb("xw_tab", [P, T], I32)
        nc.sync.dma_start(xw_tab[:], x_words[0].rearrange("p n r -> p (n r)").bitcast(I32))
        w1_raw = [load_weight_half("w1_raw%d" % h, w1, h) for h in range(2)]
        n1_l = load_list("n1_l", n1)
        w2_raw = [load_weight_half("w2_raw%d" % h, w2, h) for h in range(2)]
        k1_l = load_list("k1_l", k1)
        nc.sync.dma_start(ds_tab[0:P:8, :].bitcast(I32), d_scales[0].bitcast(I32))
        n2_l = load_list("n2_l", n2)
        n3_l = load_list("n3_l", n3)
        gs_sb = sb("gs_sb", [P, PACK], F32)
        nc.sync.dma_start(gs_sb[:], gs.rearrange("(p t) o -> p (t o)", t=PACK))
        dw_tab = sb("dw_tab", [P, G], I32)
        nc.sync.dma_start(dw_tab[:], d_words[0].rearrange("p n r -> p (n r)").bitcast(I32))
        n4_l = load_list("n4_l", n4)
        n5_l = load_list("n5_l", n5)

        def gather_bytes(name, table, lst):
            got = sb(name, [P, S], U8)
            nc.vector.tensor_copy(got[:], table[:].indirect(lst[:]))
            return got

        def gather_words(name, table, entries, count, tag=None):
            got = sb(name, [P, count], U32, tag)
            nc.vector.tensor_copy(got[:], table[:].bitcast(U32).indirect(entries))
            return got

        xa_scales = gather_bytes("xa_scales", xs_tab, offs_l)
        xb_scales = gather_bytes("xb_scales", xs_tab, two_l)
        xa_words = gather_words("xa_words", xw_tab, offs_l[:], S)
        xb_words = gather_words("xb_words", xw_tab, two_l[:], S)

        def cast_weight(name, raw):
            grouped = sb(name, [P, H * PACK], BF16)
            view = grouped[:].rearrange("p (t m j) -> p m j t", t=PACK, j=PACK)
            for h in range(2):
                nc.scalar.activation(view[:, 64 * h : 64 * (h + 1)], raw[h].rearrange("p j (m t) -> p m j t", t=PACK), COPY)
            return grouped

        def quantize(name, grouped, width):
            codes = sb(name + "_codes", [P, width], U32)
            scales = sb(name + "_scales", [P, width], U8)
            nc.vector.quantize_mx(out=codes[:].bitcast(FP8X4), scales=scales[:], in_=grouped[:])
            return codes, scales

        def product(tag, t, lhs, lhs_scales, rhs, rhs_scales, width):
            acc = psum.tile([P, S], F32, name=tag, tag=tag)
            cols = slice(P * t, P * (t + 1))
            nc.tensor.matmul_mx(out=acc[:, 0:width], lhsT=lhs[:, cols].bitcast(FP8X4), lhsT_scale=lhs_scales[:, cols],
                                rhs=rhs.bitcast(FP8X4), rhs_scale=rhs_scales, start=True, stop=True)
            return acc

        win_a = [sb("win_a%d" % t, [P, 2 * S], F32) for t in range(PACK)]
        win_b = [sb("win_b%d" % t, [P, 2 * S], F32) for t in range(PACK)]

        w1_grouped = cast_weight("w1_grouped", [r[:] for r in w1_raw])
        w1_codes, w1_scales = quantize("w1", w1_grouped, H)

        dg_scales = gather_bytes("dg_scales", ds_tab, k1_l)
        dd_scales = sb("dd_scales", [P, H], U8)
        nc.vector.tensor_copy(dd_scales[:].rearrange("p (t m) -> p m t", t=PACK), dg_scales[:].rearrange("p (m t) -> p m t", t=PACK))
        for r in range(4):
            nc.sync.dma_start(dq_scales[r:P:32, :].bitcast(I32), dd_scales[8 * r : P : 32, :].bitcast(I32))

        y_acc = [product("bank_a%d" % t, t, w1_codes, w1_scales, xa_words[:], xa_scales[:], S) for t in range(PACK)]

        def leave_y(t):
            nc.scalar.activation(win_b[t][:, S:], y_acc[t][:], COPY)
            nc.scalar.activation(win_a[t][:, 0:S], y_acc[t][:], COPY, scale=-0.5)

        w2_grouped = cast_weight("w2_grouped", [r[:] for r in w2_raw])
        w2_codes, w2_scales = quantize("w2", w2_grouped, H)
        d_acc = [product("bank_b%d" % t, t, w2_codes, w2_scales, xb_words[:], xb_scales[:], S) for t in range(PACK)]

        u, ga = {}, {}
        lo = [sb("lo%d" % t, [P, S], F32) for t in range(PACK)]
        z_grouped = [sb("z_grouped%d" % c, [P, HALF * PACK], BF16) for c in range(2)]

        def turn(tag, terms):
            acc = psum.tile([P, S], F32, name="turned", tag=tag)
            for c in range(S // P):
                cols = slice(P * c, P * (c + 1))
                for i, term in enumerate(terms):
                    nc.tensor.matmul(acc[:, cols], lhsT=term[:, cols], rhs=ident[:], is_transpose=True, start=i == 0, stop=i == len(terms) - 1)
            return acc

        def step_u(t):
            u[t] = sb("u%d" % t, [P, S], F32, None)
            nc.vector.tensor_tensor(u[t][:], win_a[t][:].indirect(n1_l[:]), win_b[t][:, S:], ALU.add)

        def step_a(t):
            ga[t] = sb("ga%d" % t, [P, S], F32)
            nc.vector.tensor_copy(ga[t][:], win_b[t][:].indirect(n2_l[:]))

        def step_min(t, c0, c1):
            nc.vector.tensor_tensor(lo[t][:, c0:c1], u[t][:, c0:c1], ga[t][:, c0:c1], ALU.min)

        def leave_z(t, values, c0, c1):
            for c in range(c0 // HALF, c1 // HALF):
                nc.scalar.activation(z_grouped[c][:].rearrange("p (n t) -> p t n", t=PACK)[:, t, :], values[:, c * HALF : (c + 1) * HALF], COPY, scale=gs_sb[:, t : t + 1])

        def step_b(t, c0, c1, tag):
            got = sb("gb%d_%d" % (t, c0), [P, c1 - c0], F32, tag)
            nc.vector.tensor_copy(got[:], win_b[t][:].indirect(n3_l[:, c0 // 16 : c1 // 16]))
            return got

        def step_max(t, c0, c1, floor, zf):
            nc.vector.tensor_tensor(zf[:, c0:c1], lo[t][:, c0:c1], floor[:], ALU.max)
            leave_z(t, zf, c0, c1)

        dg_lo = gather_words("dg_lo", dw_tab, k1_l[:, 0:16], HALF)
        last = PACK - 1
        for t in range(PACK):
            leave_y(t)
            nc.scalar.activation(win_b[t][:, 0:S], d_acc[t][:], COPY)
        zf = [sb("zf%d" % t, [P, S], F32) for t in range(PACK)]
        step_u(0)
        for t in range(last):
            step_a(t)
            floor = step_b(t, 0, S, None)
            step_min(t, 0, S)
            step_u(t + 1)
            step_max(t, 0, S, floor, zf[t])
        step_a(last)
        floor_a = step_b(last, 0, HALF, None)
        step_min(last, 0, HALF)
        step_min(last, HALF, S)
        step_max(last, 0, HALF, floor_a, zf[last])
        floor_b = step_b(last, HALF, S, "ga3")
        dq_words = sb("dq_words", [P, H], U32, "gb3_0")
        dealt = dq_words[:].rearrange("p (t m) -> p m t", t=PACK)
        nc.vector.tensor_copy(dealt[:, 0:64], dg_lo[:].rearrange("p (m t) -> p m t", t=PACK))
        step_max(last, HALF, S, floor_b, zf[last])

        dg_hi = gather_words("dg_hi", dw_tab, k1_l[:, 16:32], HALF, "win_b3")
        z_codes = sb("z_codes", [P, S], U32)
        z_scales = sb("z_scales", [P, S], U8)

        def quantize_z(c):
            cols = slice(c * HALF, (c + 1) * HALF)
            nc.vector.quantize_mx(out=z_codes[:, cols].bitcast(FP8X4), scales=z_scales[:, cols], in_=z_grouped[c][:])

        quantize_z(0)
        picked = dg_hi[:].rearrange("p (m t) -> p m t", t=PACK)
        nc.vector.tensor_copy(dealt[:, 64:128, 0:1], picked[:, :, 0:1])
        quantize_z(1)
        nc.vector.tensor_copy(dealt[:, 64:128, 1:PACK], picked[:, :, 1:PACK])
        h_first = [product(("bank_a0", "bank_b0")[c], 0, dq_words, dq_scales, z_codes[:, c * HALF : (c + 1) * HALF], z_scales[:, c * HALF : (c + 1) * HALF], HALF) for c in range(2)]
        h_acc = {t: product("bank_a%d" % t, t, dq_words, dq_scales, z_codes[:], z_scales[:], S) for t in range(1, PACK)}
        win_h = [sb("win_h%d" % t, [P, 2 * S], F32) for t in range(PACK)]
        win_st = [sb("win_st%d" % t, [P, 2 * S], F32, "win_h2" if t == 0 else None) for t in range(PACK)]
        half_h = [sb("half_h%d" % t, [P, S], F32) for t in range(PACK)]
        gh = [sb("gh%d" % t, [P, S], F32) for t in range(PACK)]
        res = [sb("res%d" % t, [P, S], F32) for t in range(PACK)]
        out_rows = out.rearrange("(p t) n -> t p n", t=PACK)
        direct, turned = (0, 3), (1, 2)

        def leave_h(t):
            nc.scalar.activation(win_h[t][:, 0:S], h_acc[t][:], COPY, scale=0.0625 if t in direct else 0.03125)

        def halve(t):
            nc.scalar.activation(half_h[t][:], win_h[t][:, 0:S], COPY, scale=0.5 if t in direct else 1.0)

        def step_h(t):
            nc.vector.tensor_copy(gh[t][:], win_h[t][:].indirect(n4_l[:]))

        def step_gap(t):
            nc.vector.tensor_tensor(gh[t][:], win_h[t][:].indirect(n4_l[:]), half_h[t][:], ALU.subtract)

        def step_st(t):
            nc.vector.tensor_tensor(win_st[t][:, 0:S], win_h[t][:, 0:S], gh[t][:], ALU.max)

        def step_out(t, c0, c1):
            nc.vector.tensor_tensor(res[t][:, c0:c1], win_st[t][:].indirect(n5_l[:, c0 // 16 : c1 // 16]), half_h[t][:, c0:c1], ALU.subtract)
            nc.sync.dma_start(out_rows[t][:, c0:c1], res[t][:, c0:c1])

        for c in range(2):
            nc.scalar.activation(win_h[0][:, c * HALF : (c + 1) * HALF], h_first[c][:, 0:HALF], COPY, scale=0.0625)
        step_h(0)
        for t in turned:
            leave_h(t)
            halve(t)
            step_gap(t)
        leave_h(last)
        step_h(last)
        rise = {}
        for t in turned:
            rise[t] = sb("rise%d" % t, [P, S], F32)
            nc.scalar.activation(rise[t][:], gh[t][:], RELU)
        for t in direct:
            step_st(t)
        halve(0)
        summed = {}
        for t in turned:
            acc = turn("bank_a%d" % t, [half_h[t], rise[t]])
            summed[t] = sb("summed%d" % t, [P, S], F32)
            nc.scalar.activation(summed[t][:], acc[:], COPY, scale=2.0)
        halve(last)
        for t in turned:
            acc = turn("bank_b%d" % t, [summed[t]])
            nc.scalar.activation(win_st[t][:, 0:S], acc[:], COPY)
        for t in direct + turned[:-1]:
            step_out(t, 0, S)
        step_out(turned[-1], 0, HALF)
        step_out(turned[-1], HALF, S)
